import numpy as np, ml_dtypes
CORES = [24,26,29,31,48,50,53,55]
N = 8
CB = 32
def setup_inputs(rng):
    return {"x": rng.standard_normal((N, 128, N * CB), dtype=np.float32).astype(ml_dtypes.bfloat16)}
def setup_inputs_big(rng):
    d = setup_inputs(rng)
    for k in ("x",): d[k] = (d[k].astype(np.float32) * 1024.0).astype(d[k].dtype)
    return d
def setup_inputs_small(rng):
    d = setup_inputs(rng)
    for k in ("x",): d[k] = (d[k].astype(np.float32) * (1 / 1024.0)).astype(d[k].dtype)
    return d
def setup_inputs_apart(rng):
    d = setup_inputs(rng)
    f = (10.0 ** rng.permutation(np.linspace(-1.5, 1.5, N))).astype(np.float32).reshape(N, 1, 1)
    for k in ("x",): d[k] = (d[k].astype(np.float32) * f).astype(d[k].dtype)
    return d
def reference(x):
    X = x.astype(np.float64)
    G = sum(X[j].T @ X[j] for j in range(N))
    y = np.full((N, CB, N * CB), np.nan)
    for r in range(N):
        y[r][:, :CB * r] = G[CB * r:CB * r + CB, :CB * r]
    return {"y": y.astype(ml_dtypes.bfloat16 if x.dtype != np.float64 else np.float64)}

@@ -1,0 +1,173 @@
+from concourse.bass import DstId, RemoteDMATransfer
+
+N = 8
+CB = 32
+KP = 128
+WID = N * CB
+
+SCRATCH = {
+    "xs": ("sbuf", [KP, WID], "bfloat16"),
+    "xin0": ("sbuf", [KP, WID], "bfloat16"),
+    "xin1": ("sbuf", [KP, WID], "bfloat16"),
+    "xin2": ("sbuf", [KP, WID], "bfloat16"),
+    "xin3": ("sbuf", [KP, WID], "bfloat16"),
+    "pat": ("sbuf", [KP, KP + 1], "bfloat16"),
+    "flat": ("dram", [KP * (KP + 1)], "bfloat16"),
+    "eye": ("sbuf", [KP, KP], "bfloat16"),
+    "piece": ("sbuf", [KP, 2, 2, CB], "bfloat16"),
+    "land": ("sbuf", [KP, 2, CB], "bfloat16"),
+    "ysb": ("sbuf", [KP, WID], "bfloat16"),
+    "acc": ("psum", [KP, 512], "float32"),
+    "pc0": ("psum", [KP, 512], "float32"),
+    "pc1": ("psum", [KP, 512], "float32"),
+}
+SEMAPHORES = ["ld", "ms", "idw", "ident", "xa0", "xa1", "xa2", "xa3", "pc", "pcs", "land", "accd", "yr", "st", "sent"]
+
+
+def _bits(mask):
+    return [b for b in range(mask.bit_length()) if (mask >> b) & 1]
+
+
+def _pick(mask, first, n):
+    return sum(1 << b for b in _bits(mask)[first:first + n])
+
+
+def _common(topo, src, dsts):
+    m = topo.mask(src, dsts[0])
+    for d in dsts[1:]:
+        m &= topo.mask(src, d)
+    return m
+
+
+def _plan(T, topo):
+    cores = list(T.cores)
+    rank = {c: i for i, c in enumerate(cores)}
+    home = {c: [d for d in cores if topo.chip(d) == topo.chip(c)] for c in cores}
+    away = {c: [d for d in cores if topo.chip(d) != topo.chip(c)] for c in cores}
+    serves = {c: [] for c in cores}
+    carrier = {}
+    for d in cores:
+        if rank[d] == 0:
+            continue
+        can = [p for p in away[d] if topo.may_write(p, d)]
+        same = [p for p in can if topo.die(p) == topo.die(d)]
+        carrier[d] = (same or can)[0]
+        serves[carrier[d]].append(d)
+    tiles = {c: max([(CB * rank[d] + KP - 1) // KP for d in serves[c]] or [0]) for c in cores}
+    need = {}
+    for c in cores:
+        w = CB * (rank[c] + 1) if rank[c] else 0
+        if serves[c]:
+            w = max(w, KP * tiles[c], CB * (max(rank[d] for d in serves[c]) + 1))
+        need[c] = w
+    xcalls = {}
+    for s in cores:
+        takers = [d for d in home[s] if d != s and need[d]]
+        calls = []
+        for grp in ([d for d in takers if serves[d]], [d for d in takers if not serves[d]]):
+            if grp:
+                calls.append((grp, max(need[d] for d in grp), _common(topo, s, grp)))
+        xcalls[s] = calls
+    share = {}
+    for p in cores:
+        if serves[p]:
+            m = _common(topo, p, serves[p])
+            n = 1
+            while n * 2 * len(serves[p]) <= len(_bits(m)):
+                n *= 2
+            share[p] = [_pick(m, i * n, n) for i in range(len(serves[p]))]
+    return rank, home, serves, carrier, tiles, xcalls, share
+
+
+def rank_program(g, core, T, topo):
+    r = T.rank_of(core)
+    if r is None:
+        return
+    rank, home, serves, carrier, tiles, xcalls, share = _plan(T, topo)
+    sem = T.sem
+    te, ve = g.tensor, g.vector
+    me = home[core].index(core)
+    mine = serves[core]
+
+    def dst_id(d):
+        rid, pid, _ = topo.addr(d)
+        return DstId(rid=rid, pnc=pid)
+
+    g.sync.dma_start(T.xs[:], T.x[:]).then_inc(sem.ld, 16)
+
+    k0 = min(KP, CB * r)
+    if r:
+        ve.memset(T.pat[0:k0, 0:1], 1.0).then_inc(sem.ms, 1)
+        ve.memset(T.pat[0:k0, 1:k0 + 1], 0.0).then_inc(sem.ms, 1)
+        g.scalar.wait_ge(sem.ms, 2)
+        g.scalar.dma_start(T.flat[0:k0 * (k0 + 1)], T.pat[0:k0, 0:k0 + 1]).then_inc(sem.idw, 16)
+        g.scalar.wait_ge(sem.idw, 16)
+        g.scalar.dma_start(T.eye[0:k0, 0:k0], T.flat[0:k0 * k0]).then_inc(sem.ident, 16)
+
+    sent = 0
+    g.wait_ge(sem.ld, 16)
+    for dsts, w, m in xcalls[core]:
+        g.remote_dma_fused(
+            [RemoteDMATransfer(dst_ids=[dst_id(d) for d in dsts], dma_engine_mask=m, remote_sem=sem["xa%d" % me],
+                               srcs=[T.xs[:, 0:w]], dsts=[T["xin%d" % me][:, 0:w] for _ in dsts], alu_op=0)],
+            local_sem=sem.sent)
+        sent += len(_bits(m))
+
+    if r or mine:
+        others = [s for s in home[core] if s != core]
+        others.sort(key=lambda s: topo.die(s) != topo.die(core))
+        srcs = [(T.xs, sem.ld, 16)]
+        for s in others:
+            cnt = [len(_bits(m)) for dsts, w, m in xcalls[s] if core in dsts][0]
+            k = home[core].index(s)
+            srcs.append((T["xin%d" % k], sem["xa%d" % k], cnt))
+        if mine:
+            lo = CB * min(rank[d] for d in mine)
+            hi = CB * (max(rank[d] for d in mine) + 1)
+            nd = (hi - lo) // CB
+        n_pc = n_acc = 0
+        for i, (xt, s_, cnt) in enumerate(srcs):
+            te.wait_ge(s_, cnt)
+            first, last = i == 0, i == len(srcs) - 1
+            if mine:
+                for t in range(tiles[core]):
+                    te.matmul(T["pc%d" % t][:, 0:hi - lo], xt[:, KP * t:KP * t + KP], xt[:, lo:hi],
+                              first, last).then_inc(sem.pc, 1)
+                    n_pc += 1
+            if r:
+                te.matmul(T.acc[0:CB, 0:CB * r], xt[:, CB * r:CB * r + CB], xt[:, 0:CB * r],
+                          first, False).then_inc(sem.accd, 1)
+                n_acc += 1
+
+    if mine:
+        nt = tiles[core]
+        ve.wait_ge(sem.pc, n_pc)
+        for t in range(nt):
+            ve.tensor_copy(T.piece[:, 0:nd, t, :], T["pc%d" % t][:, 0:hi - lo]).then_inc(sem.pcs, 1)
+        g.wait_ge(sem.pcs, nt)
+        trs = []
+        for d, m in zip(mine, share[core]):
+            slot = rank[d] - lo // CB
+            trs.append(RemoteDMATransfer(dst_ids=[dst_id(d)], dma_engine_mask=m, remote_sem=sem.land,
+                                         srcs=[T.piece[:, slot, 0:nt, :]], dsts=[T.land[:, 0:nt, :]], alu_op=0))
+            sent += len(_bits(m))
+        g.remote_dma_fused(trs, local_sem=sem.sent)
+
+    if r:
+        p = carrier[core]
+        te.wait_ge(sem.ident, 16)
+        te.wait_ge(sem.land, len(_bits(share[p][serves[p].index(core)])))
+        ntr = (CB * r + KP - 1) // KP
+        for t in range(ntr):
+            k = min(KP, CB * r - KP * t)
+            te.matmul(T.acc[0:CB, KP * t:KP * t + k], T.land[0:k, t, :], T.eye[0:k, 0:k],
+                      False, t == ntr - 1).then_inc(sem.accd, 1)
+            n_acc += 1
+        ve.wait_ge(sem.accd, n_acc)
+        ve.tensor_copy(T.ysb[0:CB, 0:CB * r], T.acc[0:CB, 0:CB * r]).then_inc(sem.yr, 1)
+        g.sync.wait_ge(sem.yr, 1)
+        g.sync.dma_start(T.y[:, 0:CB * r], T.ysb[0:CB, 0:CB * r]).then_inc(sem.st, 16)
+        g.sync.wait_ge(sem.st, 16)
+
+    if sent:
+        g.wait_ge(sem.sent, sent)

@@ -11,25 +11,27 @@ SCRATCH = {
     "xin1": ("sbuf", [KP, WID], "bfloat16"),
     "xin2": ("sbuf", [KP, WID], "bfloat16"),
     "xin3": ("sbuf", [KP, WID], "bfloat16"),
+    "pats": ("sbuf", [KP, KP + 1], "bfloat16"),
     "pat": ("sbuf", [KP, KP + 1], "bfloat16"),
     "flat": ("dram", [KP * (KP + 1)], "bfloat16"),
     "eye": ("sbuf", [KP, KP], "bfloat16"),
     "piece": ("sbuf", [KP, 2, 2, CB], "bfloat16"),
+    "piece2": ("sbuf", [KP, 2, 2, CB], "bfloat16"),
     "land": ("sbuf", [KP, 2, CB], "bfloat16"),
+    "land2": ("sbuf", [KP, 2, CB], "bfloat16"),
     "ysb": ("sbuf", [KP, WID], "bfloat16"),
     "acc": ("psum", [KP, 512], "float32"),
     "pc0": ("psum", [KP, 512], "float32"),
     "pc1": ("psum", [KP, 512], "float32"),
+    "pe0": ("psum", [KP, 512], "float32"),
+    "pe1": ("psum", [KP, 512], "float32"),
 }
-SEMAPHORES = ["ld", "ms", "idw", "ident", "xa0", "xa1", "xa2", "xa3", "pc", "pcs", "land", "accd", "yr", "st", "sent"]
+SEMAPHORES = ["ld", "ms", "pa", "idw", "ident", "xa0", "xa1", "xa2", "xa3", "pc", "pcs", "pe", "pes", "land", "land2",
+              "accd", "yr", "st", "sent"]
 
 
 def _bits(mask):
     return [b for b in range(mask.bit_length()) if (mask >> b) & 1]
-
-
-def _pick(mask, first, n):
-    return sum(1 << b for b in _bits(mask)[first:first + n])
 
 
 def _common(topo, src, dsts):
@@ -37,6 +39,14 @@ def _common(topo, src, dsts):
     for d in dsts[1:]:
         m &= topo.mask(src, d)
     return m
+
+
+def _shares(topo, src, dsts):
+    bits = _bits(_common(topo, src, dsts))
+    n = 1
+    while n * 2 * len(dsts) <= len(bits):
+        n *= 2
+    return [sum(1 << b for b in bits[i * n:i * n + n]) for i in range(len(dsts))]
 
 
 def _plan(T, topo):
@@ -53,41 +63,40 @@ def _plan(T, topo):
         same = [p for p in can if topo.die(p) == topo.die(d)]
         carrier[d] = (same or can)[0]
         serves[carrier[d]].append(d)
-    tiles = {c: max([(CB * rank[d] + KP - 1) // KP for d in serves[c]] or [0]) for c in cores}
-    need = {}
-    for c in cores:
-        w = CB * (rank[c] + 1) if rank[c] else 0
-        if serves[c]:
-            w = max(w, KP * tiles[c], CB * (max(rank[d] for d in serves[c]) + 1))
-        need[c] = w
+    direct = {c: [d for q in home[c] if q != c for d in serves[q]] if serves[c] else [] for c in cores}
+
+    def span(dsts):
+        rs = [rank[d] for d in dsts]
+        return CB * min(rs), CB * (max(rs) + 1), (CB * max(rs) + KP - 1) // KP
+
+    own = {c: CB * (rank[c] + 1) if rank[c] else 0 for c in cores}
     xcalls = {}
     for s in cores:
-        takers = [d for d in home[s] if d != s and need[d]]
+        peers = [d for d in home[s] if d != s]
         calls = []
-        for grp in ([d for d in takers if serves[d]], [d for d in takers if not serves[d]]):
+        if serves[s]:
+            groups = [([d for d in peers if own[d]], own)]
+        else:
+            full = {d: max(own[d], span(serves[d])[1], KP * span(serves[d])[2]) for d in peers if serves[d]}
+            groups = [(list(full), full), ([d for d in peers if not serves[d] and own[d]], own)]
+        for grp, w in groups:
             if grp:
-                calls.append((grp, max(need[d] for d in grp), _common(topo, s, grp)))
+                calls.append((grp, max(w[d] for d in grp), _common(topo, s, grp)))
         xcalls[s] = calls
-    share = {}
-    for p in cores:
-        if serves[p]:
-            m = _common(topo, p, serves[p])
-            n = 1
-            while n * 2 * len(serves[p]) <= len(_bits(m)):
-                n *= 2
-            share[p] = [_pick(m, i * n, n) for i in range(len(serves[p]))]
-    return rank, home, serves, carrier, tiles, xcalls, share
+    return rank, home, away, serves, carrier, direct, span, xcalls
 
 
 def rank_program(g, core, T, topo):
     r = T.rank_of(core)
     if r is None:
         return
-    rank, home, serves, carrier, tiles, xcalls, share = _plan(T, topo)
+    rank, home, away, serves, carrier, direct, span, xcalls = _plan(T, topo)
     sem = T.sem
     te, ve = g.tensor, g.vector
-    me = home[core].index(core)
-    mine = serves[core]
+    chipm = home[core]
+    me = chipm.index(core)
+    late, early = serves[core], direct[core]
+    sent = 0
 
     def dst_id(d):
         rid, pid, _ = topo.addr(d)
@@ -95,16 +104,22 @@ def rank_program(g, core, T, topo):
 
     g.sync.dma_start(T.xs[:], T.x[:]).then_inc(sem.ld, 16)
 
+    nxt, prv = chipm[(me + 1) % len(chipm)], chipm[me - 1]
+    if rank[nxt]:
+        ve.memset(T.pats[:, 0:1], 1.0).then_inc(sem.ms, 1)
+        ve.memset(T.pats[:, 1:KP + 1], 0.0).then_inc(sem.ms, 1)
+        g.wait_ge(sem.ms, 2)
+        m = topo.mask(core, nxt)
+        g.remote_dma_fused([RemoteDMATransfer(dst_ids=[dst_id(nxt)], dma_engine_mask=m, remote_sem=sem.pa,
+                                              srcs=[T.pats[:, :]], dsts=[T.pat[:, :]], alu_op=0)], local_sem=sem.sent)
+        sent += len(_bits(m))
     k0 = min(KP, CB * r)
     if r:
-        ve.memset(T.pat[0:k0, 0:1], 1.0).then_inc(sem.ms, 1)
-        ve.memset(T.pat[0:k0, 1:k0 + 1], 0.0).then_inc(sem.ms, 1)
-        g.scalar.wait_ge(sem.ms, 2)
+        g.scalar.wait_ge(sem.pa, len(_bits(topo.mask(prv, core))))
         g.scalar.dma_start(T.flat[0:k0 * (k0 + 1)], T.pat[0:k0, 0:k0 + 1]).then_inc(sem.idw, 16)
         g.scalar.wait_ge(sem.idw, 16)
         g.scalar.dma_start(T.eye[0:k0, 0:k0], T.flat[0:k0 * k0]).then_inc(sem.ident, 16)
 
-    sent = 0
     g.wait_ge(sem.ld, 16)
     for dsts, w, m in xcalls[core]:
         g.remote_dma_fused(
@@ -113,61 +128,68 @@ def rank_program(g, core, T, topo):
             local_sem=sem.sent)
         sent += len(_bits(m))
 
-    if r or mine:
-        others = [s for s in home[core] if s != core]
-        others.sort(key=lambda s: topo.die(s) != topo.die(core))
-        srcs = [(T.xs, sem.ld, 16)]
+    def tiles_of(xt, dsts, bank, first, last, s_):
+        lo, hi, nt = span(dsts)
+        for t in range(nt):
+            te.matmul(T["%s%d" % (bank, t)][:, 0:hi - lo], xt[:, KP * t:KP * t + KP], xt[:, lo:hi],
+                      first, last).then_inc(s_, 1)
+        return nt
+
+    def ship(dsts, bank, buf, n_mm, s_mm, s_cp, s_land, dst_buf):
+        lo, hi, nt = span(dsts)
+        ve.wait_ge(s_mm, n_mm)
+        for t in range(nt):
+            ve.tensor_copy(buf[:, 0:(hi - lo) // CB, t, :], T["%s%d" % (bank, t)][:, 0:hi - lo]).then_inc(s_cp, 1)
+        g.wait_ge(s_cp, nt)
+        trs = [RemoteDMATransfer(dst_ids=[dst_id(d)], dma_engine_mask=m, remote_sem=s_land,
+                                 srcs=[buf[:, rank[d] - lo // CB, 0:nt, :]], dsts=[dst_buf[:, 0:nt, :]], alu_op=0)
+               for d, m in zip(dsts, _shares(topo, core, dsts))]
+        g.remote_dma_fused(trs, local_sem=sem.sent)
+        return sum(len(_bits(m)) for m in _shares(topo, core, dsts))
+
+    n_acc = 0
+    if r or late:
+        others = [s for s in chipm if s != core]
+        others.sort(key=lambda s: (bool(serves[s]), topo.die(s) != topo.die(core)))
+        srcs = [(core, T.xs, sem.ld, 16)]
         for s in others:
             cnt = [len(_bits(m)) for dsts, w, m in xcalls[s] if core in dsts][0]
-            k = home[core].index(s)
-            srcs.append((T["xin%d" % k], sem["xa%d" % k], cnt))
-        if mine:
-            lo = CB * min(rank[d] for d in mine)
-            hi = CB * (max(rank[d] for d in mine) + 1)
-            nd = (hi - lo) // CB
-        n_pc = n_acc = 0
-        for i, (xt, s_, cnt) in enumerate(srcs):
+            k = chipm.index(s)
+            srcs.append((s, T["xin%d" % k], sem["xa%d" % k], cnt))
+        summed = [s for s, _a, _b, _c in srcs if s == core or not serves[s]]
+        n_pc = 0
+        for s, xt, s_, cnt in srcs:
             te.wait_ge(s_, cnt)
-            first, last = i == 0, i == len(srcs) - 1
-            if mine:
-                for t in range(tiles[core]):
-                    te.matmul(T["pc%d" % t][:, 0:hi - lo], xt[:, KP * t:KP * t + KP], xt[:, lo:hi],
-                              first, last).then_inc(sem.pc, 1)
-                    n_pc += 1
+            if s == core and early:
+                n_pe = tiles_of(xt, early, "pe", True, True, sem.pe)
+            if late and s in summed:
+                n_pc += tiles_of(xt, late, "pc", s == summed[0], s == summed[-1], sem.pc)
             if r:
                 te.matmul(T.acc[0:CB, 0:CB * r], xt[:, CB * r:CB * r + CB], xt[:, 0:CB * r],
-                          first, False).then_inc(sem.accd, 1)
+                          s == core, False).then_inc(sem.accd, 1)
                 n_acc += 1
 
-    if mine:
-        nt = tiles[core]
-        ve.wait_ge(sem.pc, n_pc)
-        for t in range(nt):
-            ve.tensor_copy(T.piece[:, 0:nd, t, :], T["pc%d" % t][:, 0:hi - lo]).then_inc(sem.pcs, 1)
-        g.wait_ge(sem.pcs, nt)
-        trs = []
-        for d, m in zip(mine, share[core]):
-            slot = rank[d] - lo // CB
-            trs.append(RemoteDMATransfer(dst_ids=[dst_id(d)], dma_engine_mask=m, remote_sem=sem.land,
-                                         srcs=[T.piece[:, slot, 0:nt, :]], dsts=[T.land[:, 0:nt, :]], alu_op=0))
-            sent += len(_bits(m))
-        g.remote_dma_fused(trs, local_sem=sem.sent)
+    if early:
+        sent += ship(early, "pe", T.piece2, n_pe, sem.pe, sem.pes, sem.land2, T.land2)
+    if late:
+        sent += ship(late, "pc", T.piece, n_pc, sem.pc, sem.pcs, sem.land, T.land)
 
     if r:
-        p = carrier[core]
         te.wait_ge(sem.ident, 16)
-        te.wait_ge(sem.land, len(_bits(share[p][serves[p].index(core)])))
         ntr = (CB * r + KP - 1) // KP
-        for t in range(ntr):
-            k = min(KP, CB * r - KP * t)
-            te.matmul(T.acc[0:CB, KP * t:KP * t + k], T.land[0:k, t, :], T.eye[0:k, 0:k],
-                      False, t == ntr - 1).then_inc(sem.accd, 1)
-            n_acc += 1
+        arrivals = [(q, direct[q], T.land2, sem.land2) for q in away[core] if core in direct[q]]
+        arrivals.append((carrier[core], serves[carrier[core]], T.land, sem.land))
+        for i, (q, lst, buf, s_) in enumerate(arrivals):
+            te.wait_ge(s_, len(_bits(_shares(topo, q, lst)[lst.index(core)])))
+            for t in range(ntr):
+                k = min(KP, CB * r - KP * t)
+                te.matmul(T.acc[0:CB, KP * t:KP * t + k], buf[0:k, t, :], T.eye[0:k, 0:k],
+                          False, i == len(arrivals) - 1 and t == ntr - 1).then_inc(sem.accd, 1)
+                n_acc += 1
         ve.wait_ge(sem.accd, n_acc)
         ve.tensor_copy(T.ysb[0:CB, 0:CB * r], T.acc[0:CB, 0:CB * r]).then_inc(sem.yr, 1)
         g.sync.wait_ge(sem.yr, 1)
         g.sync.dma_start(T.y[:, 0:CB * r], T.ysb[0:CB, 0:CB * r]).then_inc(sem.st, 16)
         g.sync.wait_ge(sem.st, 16)
 
-    if sent:
-        g.wait_ge(sem.sent, sent)
+    g.wait_ge(sem.sent, sent)

from concourse.bass import DstId, RemoteDMATransfer

N = 8
CB = 32
KP = 128
WID = N * CB

SCRATCH = {
    "xs": ("sbuf", [KP, WID], "bfloat16"),
    "xin0": ("sbuf", [KP, WID], "bfloat16"),
    "xin1": ("sbuf", [KP, WID], "bfloat16"),
    "xin2": ("sbuf", [KP, WID], "bfloat16"),
    "xin3": ("sbuf", [KP, WID], "bfloat16"),
    "pats": ("sbuf", [KP, KP + 1], "bfloat16"),
    "pat": ("sbuf", [KP, KP + 1], "bfloat16"),
    "flat": ("dram", [KP * (KP + 1)], "bfloat16"),
    "eye": ("sbuf", [KP, KP], "bfloat16"),
    "piece": ("sbuf", [KP, 2, 2, CB], "bfloat16"),
    "piece2": ("sbuf", [KP, 2, 2, CB], "bfloat16"),
    "land": ("sbuf", [KP, 2, CB], "bfloat16"),
    "land2": ("sbuf", [KP, 2, CB], "bfloat16"),
    "ysb": ("sbuf", [KP, WID], "bfloat16"),
    "acc": ("psum", [KP, 512], "float32"),
    "pc0": ("psum", [KP, 512], "float32"),
    "pc1": ("psum", [KP, 512], "float32"),
    "pe0": ("psum", [KP, 512], "float32"),
    "pe1": ("psum", [KP, 512], "float32"),
}
SEMAPHORES = ["ld", "ms", "pa", "idw", "ident", "xa0", "xa1", "xa2", "xa3", "pc", "pcs", "pe", "pes", "land", "land2",
              "accd", "yr", "st", "sent"]


def _bits(mask):
    return [b for b in range(mask.bit_length()) if (mask >> b) & 1]


def _common(topo, src, dsts):
    m = topo.mask(src, dsts[0])
    for d in dsts[1:]:
        m &= topo.mask(src, d)
    return m


def _shares(topo, src, dsts):
    bits = _bits(_common(topo, src, dsts))
    n = 1
    while n * 2 * len(dsts) <= len(bits):
        n *= 2
    return [sum(1 << b for b in bits[i * n:i * n + n]) for i in range(len(dsts))]


def _plan(T, topo):
    cores = list(T.cores)
    rank = {c: i for i, c in enumerate(cores)}
    home = {c: [d for d in cores if topo.chip(d) == topo.chip(c)] for c in cores}
    away = {c: [d for d in cores if topo.chip(d) != topo.chip(c)] for c in cores}
    serves = {c: [] for c in cores}
    carrier = {}
    for d in cores:
        if rank[d] == 0:
            continue
        can = [p for p in away[d] if topo.may_write(p, d)]
        same = [p for p in can if topo.die(p) == topo.die(d)]
        carrier[d] = (same or can)[0]
        serves[carrier[d]].append(d)
    direct = {c: [d for q in home[c] if q != c for d in serves[q]] if serves[c] else [] for c in cores}

    def span(dsts):
        rs = [rank[d] for d in dsts]
        return CB * min(rs), CB * (max(rs) + 1), (CB * max(rs) + KP - 1) // KP

    own = {c: CB * (rank[c] + 1) if rank[c] else 0 for c in cores}
    xcalls = {}
    for s in cores:
        peers = [d for d in home[s] if d != s]
        calls = []
        if serves[s]:
            groups = [([d for d in peers if own[d]], own)]
        else:
            full = {d: max(own[d], span(serves[d])[1], KP * span(serves[d])[2]) for d in peers if serves[d]}
            groups = [(list(full), full), ([d for d in peers if not serves[d] and own[d]], own)]
        for grp, w in groups:
            if grp:
                calls.append((grp, max(w[d] for d in grp), _common(topo, s, grp)))
        xcalls[s] = calls
    return rank, home, away, serves, carrier, direct, span, xcalls


def rank_program(g, core, T, topo):
    r = T.rank_of(core)
    if r is None:
        return
    rank, home, away, serves, carrier, direct, span, xcalls = _plan(T, topo)
    sem = T.sem
    te, ve = g.tensor, g.vector
    chipm = home[core]
    me = chipm.index(core)
    late, early = serves[core], direct[core]
    sent = 0

    def dst_id(d):
        rid, pid, _ = topo.addr(d)
        return DstId(rid=rid, pnc=pid)

    g.sync.dma_start(T.xs[:], T.x[:]).then_inc(sem.ld, 16)

    nxt, prv = chipm[(me + 1) % len(chipm)], chipm[me - 1]
    if rank[nxt]:
        ve.memset(T.pats[:, 0:1], 1.0).then_inc(sem.ms, 1)
        ve.memset(T.pats[:, 1:KP + 1], 0.0).then_inc(sem.ms, 1)
        g.wait_ge(sem.ms, 2)
        m = topo.mask(core, nxt)
        g.remote_dma_fused([RemoteDMATransfer(dst_ids=[dst_id(nxt)], dma_engine_mask=m, remote_sem=sem.pa,
                                              srcs=[T.pats[:, :]], dsts=[T.pat[:, :]], alu_op=0)], local_sem=sem.sent)
        sent += len(_bits(m))
    k0 = min(KP, CB * r)
    if r:
        g.scalar.wait_ge(sem.pa, len(_bits(topo.mask(prv, core))))
        g.scalar.dma_start(T.flat[0:k0 * (k0 + 1)], T.pat[0:k0, 0:k0 + 1]).then_inc(sem.idw, 16)
        g.scalar.wait_ge(sem.idw, 16)
        g.scalar.dma_start(T.eye[0:k0, 0:k0], T.flat[0:k0 * k0]).then_inc(sem.ident, 16)

    g.wait_ge(sem.ld, 16)
    for dsts, w, m in xcalls[core]:
        g.remote_dma_fused(
            [RemoteDMATransfer(dst_ids=[dst_id(d) for d in dsts], dma_engine_mask=m, remote_sem=sem["xa%d" % me],
                               srcs=[T.xs[:, 0:w]], dsts=[T["xin%d" % me][:, 0:w] for _ in dsts], alu_op=0)],
            local_sem=sem.sent)
        sent += len(_bits(m))

    def tiles_of(xt, dsts, bank, first, last, s_):
        lo, hi, nt = span(dsts)
        for t in range(nt):
            te.matmul(T["%s%d" % (bank, t)][:, 0:hi - lo], xt[:, KP * t:KP * t + KP], xt[:, lo:hi],
                      first, last).then_inc(s_, 1)
        return nt

    def ship(dsts, bank, buf, n_mm, s_mm, s_cp, s_land, dst_buf):
        lo, hi, nt = span(dsts)
        ve.wait_ge(s_mm, n_mm)
        for t in range(nt):
            ve.tensor_copy(buf[:, 0:(hi - lo) // CB, t, :], T["%s%d" % (bank, t)][:, 0:hi - lo]).then_inc(s_cp, 1)
        g.wait_ge(s_cp, nt)
        trs = [RemoteDMATransfer(dst_ids=[dst_id(d)], dma_engine_mask=m, remote_sem=s_land,
                                 srcs=[buf[:, rank[d] - lo // CB, 0:nt, :]], dsts=[dst_buf[:, 0:nt, :]], alu_op=0)
               for d, m in zip(dsts, _shares(topo, core, dsts))]
        g.remote_dma_fused(trs, local_sem=sem.sent)
        return sum(len(_bits(m)) for m in _shares(topo, core, dsts))

    n_acc = 0
    if r or late:
        others = [s for s in chipm if s != core]
        others.sort(key=lambda s: (bool(serves[s]), topo.die(s) != topo.die(core)))
        srcs = [(core, T.xs, sem.ld, 16)]
        for s in others:
            cnt = [len(_bits(m)) for dsts, w, m in xcalls[s] if core in dsts][0]
            k = chipm.index(s)
            srcs.append((s, T["xin%d" % k], sem["xa%d" % k], cnt))
        summed = [s for s, _a, _b, _c in srcs if s == core or not serves[s]]
        n_pc = 0
        for s, xt, s_, cnt in srcs:
            te.wait_ge(s_, cnt)
            if s == core and early:
                n_pe = tiles_of(xt, early, "pe", True, True, sem.pe)
            if late and s in summed:
                n_pc += tiles_of(xt, late, "pc", s == summed[0], s == summed[-1], sem.pc)
            if r:
                te.matmul(T.acc[0:CB, 0:CB * r], xt[:, CB * r:CB * r + CB], xt[:, 0:CB * r],
                          s == core, False).then_inc(sem.accd, 1)
                n_acc += 1

    if early:
        sent += ship(early, "pe", T.piece2, n_pe, sem.pe, sem.pes, sem.land2, T.land2)
    if late:
        sent += ship(late, "pc", T.piece, n_pc, sem.pc, sem.pcs, sem.land, T.land)

    if r:
        te.wait_ge(sem.ident, 16)
        ntr = (CB * r + KP - 1) // KP
        arrivals = [(q, direct[q], T.land2, sem.land2) for q in away[core] if core in direct[q]]
        arrivals.append((carrier[core], serves[carrier[core]], T.land, sem.land))
        for i, (q, lst, buf, s_) in enumerate(arrivals):
            te.wait_ge(s_, len(_bits(_shares(topo, q, lst)[lst.index(core)])))
            for t in range(ntr):
                k = min(KP, CB * r - KP * t)
                te.matmul(T.acc[0:CB, KP * t:KP * t + k], buf[0:k, t, :], T.eye[0:k, 0:k],
                          False, i == len(arrivals) - 1 and t == ntr - 1).then_inc(sem.accd, 1)
                n_acc += 1
        ve.wait_ge(sem.accd, n_acc)
        ve.tensor_copy(T.ysb[0:CB, 0:CB * r], T.acc[0:CB, 0:CB * r]).then_inc(sem.yr, 1)
        g.sync.wait_ge(sem.yr, 1)
        g.sync.dma_start(T.y[:, 0:CB * r], T.ysb[0:CB, 0:CB * r]).then_inc(sem.st, 16)
        g.sync.wait_ge(sem.st, 16)

    g.wait_ge(sem.sent, sent)
